import numpy as np
import ml_dtypes


def mxq(x, axis, fmt="e4m3"):
    dtype, down = {"e4m3": (ml_dtypes.float8_e4m3fn, 7), "e5m2": (ml_dtypes.float8_e5m2, 14)}[fmt]
    v = np.moveaxis(np.asarray(x, np.float32).astype(ml_dtypes.bfloat16).astype(np.float64), axis, -1)
    blocks = v.reshape(v.shape[:-1] + (-1, 32))
    amax = np.abs(blocks).max(-1, keepdims=True)
    byte = np.maximum(np.where(amax > 0, np.frexp(amax)[1] - 1 + 127, 0) - down, 1)
    scale = np.exp2(byte - 127.0)
    codes = (blocks / scale).astype(np.float32).astype(dtype).astype(np.float64)
    return np.moveaxis((codes * scale).reshape(v.shape), -1, axis)


WIDE = False


def mx_kscale(k):
    if not WIDE:
        return np.ones(k)
    levels = np.array([10, -10, 5, -5, 0])
    if k % 512:
        return np.exp2(np.random.permutation(np.resize(levels, k // 32))).repeat(32)
    a = np.empty((k // 512, 16))
    for p in range(k // 512):
        a[p, :8] = np.random.permutation(np.resize(levels, 8))
        for g in range(8):
            far = levels[np.abs(levels - a[p, g]) >= 10]
            a[p, g + 8] = far[np.random.randint(len(far))]
    return np.exp2(a.ravel()).repeat(32)


def f64(x):
    return np.asarray(x).astype(np.float64)


def striped(idx):
    return np.tile(np.asarray(idx).reshape(-1, 16).T, (8, 1)).astype(np.uint16)


def unstriped(offs):
    return offs[:16].T.reshape(-1).astype(np.int64)


E2M1 = np.array([0.0, 0.5, 1.0, 1.5, 2.0, 3.0, 4.0, 6.0, -0.0, -0.5, -1.0, -1.5, -2.0, -3.0, -4.0, -6.0])


def pack_weight(w, fmt):
    k, n = w.shape
    w = f64(np.asarray(w, np.float32).astype(ml_dtypes.bfloat16)).reshape(k // 32, 32, n)
    amax = np.abs(w).max(1)
    if fmt == "e4m3":
        byte = np.frexp(amax)[1] - 1 + 127 - 7
    else:
        mant, ex = np.frexp(amax / 6.0)
        byte = np.where(mant > 0.5, ex, ex - 1) + 127
    byte = np.clip(np.where(amax > 0, byte, 1), 1, 254)
    scaled = (w * np.exp2(127.0 - byte)[:, None, :]).reshape(k, n).astype(np.float32)
    by_word = np.ascontiguousarray(scaled.reshape(k // 512, 128, 4, n).transpose(0, 1, 3, 2))
    if fmt == "e4m3":
        words = by_word.astype(ml_dtypes.float8_e4m3fn).view(np.uint8)
    else:
        c = by_word.astype(ml_dtypes.float4_e2m1fn).view(np.uint8) & 0xF
        words = (c[..., 0::2] | (c[..., 1::2] << 4)).reshape(k // 512, 128, 2 * n)
    return np.ascontiguousarray(words), np.ascontiguousarray(byte.astype(np.uint8).reshape(k // 512, 16, n))


def unpack_weight(words, scales, fmt):
    g, _, n = scales.shape
    words = np.ascontiguousarray(words).reshape(g, 128, n, -1)
    if fmt == "e4m3":
        vals = words.view(ml_dtypes.float8_e4m3fn).astype(np.float64)
    else:
        nib = np.empty((g, 128, n, 4), np.uint8)
        nib[..., 0::2] = words & 0xF
        nib[..., 1::2] = words >> 4
        vals = E2M1[nib]
    vals = vals * np.repeat(np.exp2(scales.astype(np.float64) - 127.0), 8, axis=1)[..., None]
    return vals.transpose(0, 1, 3, 2).reshape(g * 512, n)


def sigmoid(v):
    return 1.0 / (1.0 + np.exp(-v))


def bf(x):
    return np.asarray(x, np.float32).astype(ml_dtypes.bfloat16)


def planes(Y):
    r, m = Y.shape
    b = f64(bf(Y)).reshape(r // 32, 32, m)
    amax = np.abs(b).max(1)
    byte = np.clip(np.where(amax > 0, np.frexp(amax)[1] - 1 + 127 - 7, 1), 1, 254)
    codes = (b * np.exp2(127.0 - byte)[:, None, :]).reshape(r, m).astype(np.float32).astype(ml_dtypes.float8_e4m3fn).view(np.uint8)
    words = codes.reshape(r // 512, 128, 4, m).transpose(0, 1, 3, 2)
    return np.ascontiguousarray(words), np.ascontiguousarray(byte.astype(np.uint8).reshape(r // 512, 16, m))


K, T, J, N, C = 1024, 2048, 512, 512, 512


def setup_inputs():
    n = np.random.standard_normal
    idx = np.random.permutation(T)[:J]
    fk = mx_kscale(K)
    wvp = pack_weight(n((K, N)) * 1 / np.sqrt(K) * fk[:, None], "e2m1")
    wcp = pack_weight(n((K, C)) * 0.5 / np.sqrt(K) * fk[:, None], "e4m3")
    return {
        "xt": (n((K, T)) * np.random.uniform(0.3, 1.7, (1, T)) / fk[:, None]).astype(np.float32),
        "wv_words": wvp[0],
        "wv_scales": wvp[1],
        "wc_words": wcp[0],
        "wc_scales": wcp[1],
        "offs": striped(idx),
    }


def reference(xt, wv_words, wv_scales, wc_words, wc_scales, offs):
    idx = unstriped(offs)
    wvu = unpack_weight(wv_words, wv_scales, "e2m1")
    wcu = unpack_weight(wc_words, wc_scales, "e4m3")
    xtidxq = mxq(f64(xt)[:, idx], 0, "e4m3")
    v = xtidxq.T @ wvu
    a = xtidxq.T @ wcu
    y = v * sigmoid(np.max(a, axis=1, keepdims=True) - 1.0)
    words, scales = planes(y)
    return y, words, scales

@@ -1,0 +1,165 @@
+from contextlib import ExitStack
+
+import concourse.mybir as mybir
+
+K, T, J, N = 1024, 2048, 512, 512
+FLOPS = 2 * 2 * K * J * N
+
+F32 = mybir.dt.float32
+BF16 = mybir.dt.bfloat16
+I32 = mybir.dt.int32
+U32 = mybir.dt.uint32
+U16 = mybir.dt.uint16
+U8 = mybir.dt.uint8
+FP8X4 = mybir.dt.float8_e4m3fn_x4
+FP4X4 = mybir.dt.float4_e2m1fn_x4
+ACT = mybir.ActivationFunctionType
+ALU = mybir.AluOpType
+
+P = 128
+PACK = 4
+PASSES = K // (P * PACK)
+QUADRANTS = 4
+HALF = N // 2
+
+
+def tile_moe_expert_gated_by_confidence_pl_kernel(
+    tc, xt, wv_words, wv_scales, wc_words, wc_scales, offs, out_0, out_1, out_2
+):
+    nc = tc.nc
+    with ExitStack() as ctx:
+        sb = ctx.enter_context(tc.tile_pool(name="sb", bufs=1))
+        ps = ctx.enter_context(tc.psum_pool(name="ps", bufs=1))
+
+        offsets = sb.tile([P, J // 16], U16, name="offsets")
+        x_rows = [[sb.tile([P, T], F32, name="x_%d_%d" % (g, r)) for r in range(PACK)] for g in range(PASSES)]
+        wv = [sb.tile([P, 2 * N], U8, name="wv_%d" % g, align_bytes=64) for g in range(PASSES)]
+        wc = [sb.tile([P, 4 * N], U8, name="wc_%d" % g, align_bytes=64) for g in range(PASSES)]
+        wv_sc = sb.tile([P, PASSES, N], U8, name="wv_sc", align_bytes=64)
+        wc_sc = sb.tile([P, PASSES, N], U8, name="wc_sc", align_bytes=64)
+
+        def load_x(g, r):
+            rows = xt[g * P * PACK : (g + 1) * P * PACK, :].rearrange("(p r) t -> p r t", r=PACK)
+            nc.sync.dma_start(out=x_rows[g][r][:], in_=rows[:, r, :])
+
+        def load_wv(g):
+            nc.sync.dma_start(out=wv[g][:].bitcast(I32), in_=wv_words[g].bitcast(I32))
+
+        def load_wc(g):
+            nc.sync.dma_start(out=wc[g][:].bitcast(I32), in_=wc_words[g].rearrange("p n t -> p (n t)").bitcast(I32))
+
+        warm = sb.tile([P, 8], F32, name="warm")
+        nc.vector.memset(warm[:, 0:1], 0.0)
+        for plane in (wv_sc, wc_sc):
+            nc.vector.memset(plane[:].rearrange("p g n -> p (g n)").bitcast(I32), 0)
+        nc.scalar.activation(out=warm[:, 1:2], in_=warm[:, 0:1], func=ACT.Sigmoid)
+
+        load_x(0, 0)
+        nc.sync.dma_start(offsets[:], offs)
+        for plane, scales in ((wv_sc, wv_scales), (wc_sc, wc_scales)):
+            for q in range(QUADRANTS):
+                nc.scalar.dma_start(
+                    out=plane[32 * q : 32 * q + 4, :, :].bitcast(I32),
+                    in_=scales[:, 4 * q : 4 * q + 4, :].rearrange("g q n -> q g n").bitcast(I32),
+                )
+        for r in range(1, PACK):
+            load_x(0, r)
+        for r in range(PACK - 1):
+            load_x(1, r)
+        load_wv(0)
+        load_x(1, PACK - 1)
+        load_wc(0)
+        load_wc(1)
+        load_wv(1)
+
+        x_codes = []
+        x_scales = []
+        for g in range(PASSES):
+            grouped = sb.tile([P, PACK, P, PACK], BF16, name="grouped_%d" % g, align_bytes=64)
+            dealt = grouped[:].rearrange("p s m r -> p m s r")
+            for r in range(PACK):
+                nc.vector.tensor_copy(out=dealt[:, :, :, r], in_=x_rows[g][r][:].indirect(offsets[:]))
+            codes = sb.tile([P, PACK, P], U32, name="x_codes_%d" % g, align_bytes=64)
+            scale_plane = sb.tile([P, PACK, P], U8, name="x_scales_%d" % g, align_bytes=64)
+            for s in range(PACK):
+                nc.vector.quantize_mx(
+                    out=codes[:, s, :].bitcast(FP8X4),
+                    scales=scale_plane[:, s, :],
+                    in_=grouped[:, s, :, :].rearrange("p m r -> p (m r)"),
+                )
+            x_codes.append(codes)
+            x_scales.append(scale_plane)
+
+        v_ps = [ps.tile([P, N], F32, name="v_%d" % s) for s in range(PACK)]
+        a_ps = [ps.tile([P, N], F32, name="a_%d" % s) for s in range(PACK)]
+
+        def product(acc, s, g, words, plane):
+            nc.tensor.matmul_mx(
+                out=acc[:],
+                lhsT=x_codes[g][:, s, :].bitcast(FP8X4),
+                lhsT_scale=x_scales[g][:, s, :],
+                rhs=words,
+                rhs_scale=plane[:, g, :],
+                start=(g == 0),
+                stop=(g == PASSES - 1),
+            )
+
+        def values(s, g):
+            product(v_ps[s], s, g, wv[g][:].bitcast(FP4X4), wv_sc)
+
+        def scores(s, g):
+            product(a_ps[s], s, g, wc[g][:].bitcast(FP8X4), wc_sc)
+
+        for s in range(PACK):
+            values(s, 0)
+        for s in range(PACK):
+            scores(s, 0)
+        scores(0, 1)
+        for s in range(1, PACK):
+            scores(s, 1)
+            values(s - 1, 1)
+        values(PACK - 1, 1)
+
+        top = sb.tile([P, PACK], F32, name="top")
+        gate = sb.tile([P, PACK], F32, name="gate")
+        y_all = sb.tile([P, PACK, N], F32, name="y_all")
+        out_rows = out_0.rearrange("(p s) n -> p s n", s=PACK)
+        for s in range(PACK):
+            nc.vector.tensor_reduce(out=top[:, s : s + 1], in_=a_ps[s][:], axis=mybir.AxisListType.X, op=ALU.max)
+            nc.scalar.activation(out=gate[:, s : s + 1], in_=top[:, s : s + 1], func=ACT.Sigmoid, bias=-1.0)
+            if s != 2:
+                nc.scalar.activation(out=y_all[:, s, :], in_=v_ps[s][:], func=ACT.Copy, scale=gate[:, s : s + 1])
+                nc.sync.dma_start(out=out_rows[:, s, :], in_=y_all[:, s, :])
+        nc.vector.tensor_scalar(
+            out=y_all[:, 2, :], in0=v_ps[2][:], scalar1=gate[:, 2:3], scalar2=None, op0=ALU.mult
+        )
+        nc.sync.dma_start(out=out_rows[:, 2, :], in_=y_all[:, 2, :])
+
+        y_words = sb.tile([P, N], U32, name="y_words", align_bytes=64)
+        y_scales = sb.tile([P, N], U8, name="y_scales", align_bytes=64)
+        words_out = out_1[0].rearrange("p n t -> p (n t)").bitcast(I32)
+        y_bf = []
+        for h in range(2):
+            cols = slice(h * HALF, (h + 1) * HALF)
+            half = sb.tile([P, HALF, PACK], BF16, name="y_bf_%d" % h, align_bytes=64)
+            dst = half[:].rearrange("p (c i) s -> p c s i", i=4)
+            src = y_all[:, :, cols].rearrange("p s (c i) -> p c s i", i=4)
+            if h == 0:
+                nc.vector.tensor_copy(out=dst, in_=src)
+            else:
+                nc.scalar.copy(out=dst, in_=src)
+            y_bf.append(half)
+        for h in range(2):
+            cols = slice(h * HALF, (h + 1) * HALF)
+            nc.vector.quantize_mx(
+                out=y_words[:, cols].bitcast(FP8X4),
+                scales=y_scales[:, cols],
+                in_=y_bf[h][:].rearrange("p n s -> p (n s)"),
+            )
+            nc.sync.dma_start(out=words_out[:, cols], in_=y_words[:, cols].bitcast(I32))
+        for q in range(QUADRANTS):
+            queue = nc.sync if q % 2 == 0 else nc.scalar
+            queue.dma_start(
+                out=out_2[0, 4 * q : 4 * q + 4, :].bitcast(I32),
+                in_=y_scales[32 * q : 32 * q + 4, :].bitcast(I32),
+            )

@@ -21,6 +21,7 @@ PACK = 4
 PASSES = K // (P * PACK)
 QUADRANTS = 4
 HALF = N // 2
+VECTOR_SHARE = 64
 
 
 def tile_moe_expert_gated_by_confidence_pl_kernel(
@@ -48,6 +49,13 @@ def tile_moe_expert_gated_by_confidence_pl_kernel(
         def load_wc(g):
             nc.sync.dma_start(out=wc[g][:].bitcast(I32), in_=wc_words[g].rearrange("p n t -> p (n t)").bitcast(I32))
 
+        def load_scales(plane, scales):
+            for q in range(QUADRANTS):
+                nc.sync.dma_start(
+                    out=plane[32 * q : 32 * q + 4, :, :].bitcast(I32),
+                    in_=scales[:, 4 * q : 4 * q + 4, :].rearrange("g q n -> q g n").bitcast(I32),
+                )
+
         warm = sb.tile([P, 8], F32, name="warm")
         nc.vector.memset(warm[:, 0:1], 0.0)
         for plane in (wv_sc, wc_sc):
@@ -56,18 +64,14 @@ def tile_moe_expert_gated_by_confidence_pl_kernel(
 
         load_x(0, 0)
         nc.sync.dma_start(offsets[:], offs)
-        for plane, scales in ((wv_sc, wv_scales), (wc_sc, wc_scales)):
-            for q in range(QUADRANTS):
-                nc.scalar.dma_start(
-                    out=plane[32 * q : 32 * q + 4, :, :].bitcast(I32),
-                    in_=scales[:, 4 * q : 4 * q + 4, :].rearrange("g q n -> q g n").bitcast(I32),
-                )
         for r in range(1, PACK):
             load_x(0, r)
         for r in range(PACK - 1):
             load_x(1, r)
+        load_scales(wv_sc, wv_scales)
         load_wv(0)
         load_x(1, PACK - 1)
+        load_scales(wc_sc, wc_scales)
         load_wc(0)
         load_wc(1)
         load_wv(1)
@@ -127,28 +131,32 @@ def tile_moe_expert_gated_by_confidence_pl_kernel(
         for s in range(PACK):
             nc.vector.tensor_reduce(out=top[:, s : s + 1], in_=a_ps[s][:], axis=mybir.AxisListType.X, op=ALU.max)
             nc.scalar.activation(out=gate[:, s : s + 1], in_=top[:, s : s + 1], func=ACT.Sigmoid, bias=-1.0)
-            if s != 2:
+            if s < 2:
                 nc.scalar.activation(out=y_all[:, s, :], in_=v_ps[s][:], func=ACT.Copy, scale=gate[:, s : s + 1])
                 nc.sync.dma_start(out=out_rows[:, s, :], in_=y_all[:, s, :])
         nc.vector.tensor_scalar(
             out=y_all[:, 2, :], in0=v_ps[2][:], scalar1=gate[:, 2:3], scalar2=None, op0=ALU.mult
         )
         nc.sync.dma_start(out=out_rows[:, 2, :], in_=y_all[:, 2, :])
+        for h in range(2):
+            cols = slice(h * HALF, (h + 1) * HALF)
+            nc.scalar.activation(out=y_all[:, 3, cols], in_=v_ps[3][:, cols], func=ACT.Copy, scale=gate[:, 3:4])
+        nc.sync.dma_start(out=out_rows[:, 3, :], in_=y_all[:, 3, :])
 
         y_words = sb.tile([P, N], U32, name="y_words", align_bytes=64)
         y_scales = sb.tile([P, N], U8, name="y_scales", align_bytes=64)
         words_out = out_1[0].rearrange("p n t -> p (n t)").bitcast(I32)
-        y_bf = []
-        for h in range(2):
-            cols = slice(h * HALF, (h + 1) * HALF)
-            half = sb.tile([P, HALF, PACK], BF16, name="y_bf_%d" % h, align_bytes=64)
-            dst = half[:].rearrange("p (c i) s -> p c s i", i=4)
-            src = y_all[:, :, cols].rearrange("p s (c i) -> p c s i", i=4)
-            if h == 0:
-                nc.vector.tensor_copy(out=dst, in_=src)
-            else:
-                nc.scalar.copy(out=dst, in_=src)
-            y_bf.append(half)
+        y_bf = [sb.tile([P, HALF, PACK], BF16, name="y_bf_%d" % h, align_bytes=64) for h in range(2)]
+
+        def regroup(copy, h, first, last):
+            copy(
+                out=y_bf[h][:, first:last, :].rearrange("p (c i) s -> p c s i", i=4),
+                in_=y_all[:, :, h * HALF + first : h * HALF + last].rearrange("p s (c i) -> p c s i", i=4),
+            )
+
+        regroup(nc.vector.tensor_copy, 0, 0, HALF)
+        regroup(nc.scalar.copy, 1, VECTOR_SHARE, HALF)
+        regroup(nc.vector.tensor_copy, 1, 0, VECTOR_SHARE)
         for h in range(2):
             cols = slice(h * HALF, (h + 1) * HALF)
             nc.vector.quantize_mx(

@@ -51,7 +51,7 @@ def tile_moe_expert_gated_by_confidence_pl_kernel(
 
         def load_scales(plane, scales):
             for q in range(QUADRANTS):
-                nc.sync.dma_start(
+                nc.scalar.dma_start(
                     out=plane[32 * q : 32 * q + 4, :, :].bitcast(I32),
                     in_=scales[:, 4 * q : 4 * q + 4, :].rearrange("g q n -> q g n").bitcast(I32),
                 )
@@ -64,14 +64,14 @@ def tile_moe_expert_gated_by_confidence_pl_kernel(
 
         load_x(0, 0)
         nc.sync.dma_start(offsets[:], offs)
+        load_scales(wv_sc, wv_scales)
+        load_scales(wc_sc, wc_scales)
         for r in range(1, PACK):
             load_x(0, r)
         for r in range(PACK - 1):
             load_x(1, r)
-        load_scales(wv_sc, wv_scales)
         load_wv(0)
         load_x(1, PACK - 1)
-        load_scales(wc_sc, wc_scales)
         load_wc(0)
         load_wc(1)
         load_wv(1)
@@ -81,7 +81,16 @@ def tile_moe_expert_gated_by_confidence_pl_kernel(
         for g in range(PASSES):
             grouped = sb.tile([P, PACK, P, PACK], BF16, name="grouped_%d" % g, align_bytes=64)
             dealt = grouped[:].rearrange("p s m r -> p m s r")
-            for r in range(PACK):
+            staged = PACK if g == 0 else PACK // 2
+            picked = sb.tile([P, staged, J], F32, name="picked_%d" % g)
+            for r in range(staged):
+                nc.vector.tensor_copy(out=picked[:, r, :], in_=x_rows[g][r][:].indirect(offsets[:]))
+            weave = nc.scalar.copy if g == 0 else nc.vector.tensor_copy
+            weave(
+                out=grouped[:, :, :, 0:staged].rearrange("p s m r -> p m r s"),
+                in_=picked[:].rearrange("p r (m s) -> p m r s", s=PACK),
+            )
+            for r in range(staged, PACK):
                 nc.vector.tensor_copy(out=dealt[:, :, :, r], in_=x_rows[g][r][:].indirect(offsets[:]))
             codes = sb.tile([P, PACK, P], U32, name="x_codes_%d" % g, align_bytes=64)
             scale_plane = sb.tile([P, PACK, P], U8, name="x_scales_%d" % g, align_bytes=64)

from contextlib import ExitStack

import concourse.mybir as mybir

K, T, J, N = 1024, 2048, 512, 512
FLOPS = 2 * 2 * K * J * N

F32 = mybir.dt.float32
BF16 = mybir.dt.bfloat16
I32 = mybir.dt.int32
U32 = mybir.dt.uint32
U16 = mybir.dt.uint16
U8 = mybir.dt.uint8
FP8X4 = mybir.dt.float8_e4m3fn_x4
FP4X4 = mybir.dt.float4_e2m1fn_x4
ACT = mybir.ActivationFunctionType
ALU = mybir.AluOpType

P = 128
PACK = 4
PASSES = K // (P * PACK)
QUADRANTS = 4
HALF = N // 2
VECTOR_SHARE = 64


def tile_moe_expert_gated_by_confidence_pl_kernel(
    tc, xt, wv_words, wv_scales, wc_words, wc_scales, offs, out_0, out_1, out_2
):
    nc = tc.nc
    with ExitStack() as ctx:
        sb = ctx.enter_context(tc.tile_pool(name="sb", bufs=1))
        ps = ctx.enter_context(tc.psum_pool(name="ps", bufs=1))

        offsets = sb.tile([P, J // 16], U16, name="offsets")
        x_rows = [[sb.tile([P, T], F32, name="x_%d_%d" % (g, r)) for r in range(PACK)] for g in range(PASSES)]
        wv = [sb.tile([P, 2 * N], U8, name="wv_%d" % g, align_bytes=64) for g in range(PASSES)]
        wc = [sb.tile([P, 4 * N], U8, name="wc_%d" % g, align_bytes=64) for g in range(PASSES)]
        wv_sc = sb.tile([P, PASSES, N], U8, name="wv_sc", align_bytes=64)
        wc_sc = sb.tile([P, PASSES, N], U8, name="wc_sc", align_bytes=64)

        def load_x(g, r):
            rows = xt[g * P * PACK : (g + 1) * P * PACK, :].rearrange("(p r) t -> p r t", r=PACK)
            nc.sync.dma_start(out=x_rows[g][r][:], in_=rows[:, r, :])

        def load_wv(g):
            nc.sync.dma_start(out=wv[g][:].bitcast(I32), in_=wv_words[g].bitcast(I32))

        def load_wc(g):
            nc.sync.dma_start(out=wc[g][:].bitcast(I32), in_=wc_words[g].rearrange("p n t -> p (n t)").bitcast(I32))

        def load_scales(plane, scales):
            for q in range(QUADRANTS):
                nc.scalar.dma_start(
                    out=plane[32 * q : 32 * q + 4, :, :].bitcast(I32),
                    in_=scales[:, 4 * q : 4 * q + 4, :].rearrange("g q n -> q g n").bitcast(I32),
                )

        warm = sb.tile([P, 8], F32, name="warm")
        nc.vector.memset(warm[:, 0:1], 0.0)
        for plane in (wv_sc, wc_sc):
            nc.vector.memset(plane[:].rearrange("p g n -> p (g n)").bitcast(I32), 0)
        nc.scalar.activation(out=warm[:, 1:2], in_=warm[:, 0:1], func=ACT.Sigmoid)

        load_x(0, 0)
        nc.sync.dma_start(offsets[:], offs)
        load_scales(wv_sc, wv_scales)
        load_scales(wc_sc, wc_scales)
        for r in range(1, PACK):
            load_x(0, r)
        for r in range(PACK - 1):
            load_x(1, r)
        load_wv(0)
        load_x(1, PACK - 1)
        load_wc(0)
        load_wc(1)
        load_wv(1)

        x_codes = []
        x_scales = []
        for g in range(PASSES):
            grouped = sb.tile([P, PACK, P, PACK], BF16, name="grouped_%d" % g, align_bytes=64)
            dealt = grouped[:].rearrange("p s m r -> p m s r")
            staged = PACK if g == 0 else PACK // 2
            picked = sb.tile([P, staged, J], F32, name="picked_%d" % g)
            for r in range(staged):
                nc.vector.tensor_copy(out=picked[:, r, :], in_=x_rows[g][r][:].indirect(offsets[:]))
            weave = nc.scalar.copy if g == 0 else nc.vector.tensor_copy
            weave(
                out=grouped[:, :, :, 0:staged].rearrange("p s m r -> p m r s"),
                in_=picked[:].rearrange("p r (m s) -> p m r s", s=PACK),
            )
            for r in range(staged, PACK):
                nc.vector.tensor_copy(out=dealt[:, :, :, r], in_=x_rows[g][r][:].indirect(offsets[:]))
            codes = sb.tile([P, PACK, P], U32, name="x_codes_%d" % g, align_bytes=64)
            scale_plane = sb.tile([P, PACK, P], U8, name="x_scales_%d" % g, align_bytes=64)
            for s in range(PACK):
                nc.vector.quantize_mx(
                    out=codes[:, s, :].bitcast(FP8X4),
                    scales=scale_plane[:, s, :],
                    in_=grouped[:, s, :, :].rearrange("p m r -> p (m r)"),
                )
            x_codes.append(codes)
            x_scales.append(scale_plane)

        v_ps = [ps.tile([P, N], F32, name="v_%d" % s) for s in range(PACK)]
        a_ps = [ps.tile([P, N], F32, name="a_%d" % s) for s in range(PACK)]

        def product(acc, s, g, words, plane):
            nc.tensor.matmul_mx(
                out=acc[:],
                lhsT=x_codes[g][:, s, :].bitcast(FP8X4),
                lhsT_scale=x_scales[g][:, s, :],
                rhs=words,
                rhs_scale=plane[:, g, :],
                start=(g == 0),
                stop=(g == PASSES - 1),
            )

        def values(s, g):
            product(v_ps[s], s, g, wv[g][:].bitcast(FP4X4), wv_sc)

        def scores(s, g):
            product(a_ps[s], s, g, wc[g][:].bitcast(FP8X4), wc_sc)

        for s in range(PACK):
            values(s, 0)
        for s in range(PACK):
            scores(s, 0)
        scores(0, 1)
        for s in range(1, PACK):
            scores(s, 1)
            values(s - 1, 1)
        values(PACK - 1, 1)

        top = sb.tile([P, PACK], F32, name="top")
        gate = sb.tile([P, PACK], F32, name="gate")
        y_all = sb.tile([P, PACK, N], F32, name="y_all")
        out_rows = out_0.rearrange("(p s) n -> p s n", s=PACK)
        for s in range(PACK):
            nc.vector.tensor_reduce(out=top[:, s : s + 1], in_=a_ps[s][:], axis=mybir.AxisListType.X, op=ALU.max)
            nc.scalar.activation(out=gate[:, s : s + 1], in_=top[:, s : s + 1], func=ACT.Sigmoid, bias=-1.0)
            if s < 2:
                nc.scalar.activation(out=y_all[:, s, :], in_=v_ps[s][:], func=ACT.Copy, scale=gate[:, s : s + 1])
                nc.sync.dma_start(out=out_rows[:, s, :], in_=y_all[:, s, :])
        nc.vector.tensor_scalar(
            out=y_all[:, 2, :], in0=v_ps[2][:], scalar1=gate[:, 2:3], scalar2=None, op0=ALU.mult
        )
        nc.sync.dma_start(out=out_rows[:, 2, :], in_=y_all[:, 2, :])
        for h in range(2):
            cols = slice(h * HALF, (h + 1) * HALF)
            nc.scalar.activation(out=y_all[:, 3, cols], in_=v_ps[3][:, cols], func=ACT.Copy, scale=gate[:, 3:4])
        nc.sync.dma_start(out=out_rows[:, 3, :], in_=y_all[:, 3, :])

        y_words = sb.tile([P, N], U32, name="y_words", align_bytes=64)
        y_scales = sb.tile([P, N], U8, name="y_scales", align_bytes=64)
        words_out = out_1[0].rearrange("p n t -> p (n t)").bitcast(I32)
        y_bf = [sb.tile([P, HALF, PACK], BF16, name="y_bf_%d" % h, align_bytes=64) for h in range(2)]

        def regroup(copy, h, first, last):
            copy(
                out=y_bf[h][:, first:last, :].rearrange("p (c i) s -> p c s i", i=4),
                in_=y_all[:, :, h * HALF + first : h * HALF + last].rearrange("p s (c i) -> p c s i", i=4),
            )

        regroup(nc.vector.tensor_copy, 0, 0, HALF)
        regroup(nc.scalar.copy, 1, VECTOR_SHARE, HALF)
        regroup(nc.vector.tensor_copy, 1, 0, VECTOR_SHARE)
        for h in range(2):
            cols = slice(h * HALF, (h + 1) * HALF)
            nc.vector.quantize_mx(
                out=y_words[:, cols].bitcast(FP8X4),
                scales=y_scales[:, cols],
                in_=y_bf[h][:].rearrange("p n s -> p (n s)"),
            )
            nc.sync.dma_start(out=words_out[:, cols], in_=y_words[:, cols].bitcast(I32))
        for q in range(QUADRANTS):
            queue = nc.sync if q % 2 == 0 else nc.scalar
            queue.dma_start(
                out=out_2[0, 4 * q : 4 * q + 4, :].bitcast(I32),
                in_=y_scales[32 * q : 32 * q + 4, :].bitcast(I32),
            )
